import numpy as np, ml_dtypes
CORES = [52,68,84,180,196,212,308,324,340]
N = 9
KB, QP, ROOT = 4, 128, 0
def setup_inputs(rng):
    return {"q": rng.standard_normal((N, 128, QP), dtype=np.float32).astype(ml_dtypes.bfloat16), "k": rng.standard_normal((N, 128, KB * 128), dtype=np.float32).astype(ml_dtypes.bfloat16), "v": rng.standard_normal((N, 128, KB * 128), dtype=np.float32).astype(ml_dtypes.bfloat16)}
def setup_inputs_big(rng):
    d = setup_inputs(rng)
    for k in ("q", "k", "v"): d[k] = (d[k].astype(np.float32) * 1024.0).astype(d[k].dtype)
    return d
def setup_inputs_small(rng):
    d = setup_inputs(rng)
    for k in ("q", "k", "v"): d[k] = (d[k].astype(np.float32) * (1 / 1024.0)).astype(d[k].dtype)
    return d
def setup_inputs_apart(rng):
    d = setup_inputs(rng)
    f = (10.0 ** rng.permutation(np.linspace(-1.5, 1.5, N))).astype(np.float32).reshape(N, 1, 1)
    for k in ("q", "k", "v"): d[k] = (d[k].astype(np.float32) * f).astype(d[k].dtype)
    return d
def reference(q, k, v):
    Q, K, V = q.astype(np.float64), k.astype(np.float64), v.astype(np.float64)
    o = np.zeros((128, QP))
    for j in range(N):
        for b in range(KB):
            o += V[j][:, 128 * b:128 * b + 128].T @ np.maximum(K[j][:, 128 * b:128 * b + 128].T @ Q[ROOT], 0.0)
    y = np.full((N, 128, QP), np.nan)
    y[ROOT] = o
    return {"y": y.astype(ml_dtypes.bfloat16 if q.dtype != np.float64 else np.float64)}

@@ -1,0 +1,141 @@
+from concourse.bass import DstId, RemoteDMATransfer
+from concourse.mybir import AluOpType
+
+KB = 4
+W = 128
+NBANK = 4
+MAXB = 2 * KB
+NSLOT = 5
+
+SCRATCH = {
+    "qs": ("sbuf", [128, W], "bfloat16"),
+    "ks": ("sbuf", [128, MAXB * W], "bfloat16"),
+    "vs": ("sbuf", [128, MAXB * W], "bfloat16"),
+    "zero": ("sbuf", [128, W], "float32"),
+    "ss": ("sbuf", [128, MAXB * W], "bfloat16"),
+    "ob": ("sbuf", [128, W], "bfloat16"),
+    "land": ("sbuf", [128, NSLOT * W], "bfloat16"),
+    "ps0": ("psum", [128, 512], "float32"),
+    "ps1": ("psum", [128, 512], "float32"),
+    "ps2": ("psum", [128, 512], "float32"),
+    "ps3": ("psum", [128, 512], "float32"),
+    "po": ("psum", [128, 512], "float32"),
+}
+SEMAPHORES = (["q_in", "ld_k", "ld_v", "k2_in", "v2_in", "sent", "zf", "o_done", "o_rdy", "st"]
+              + ["s%d" % b for b in range(MAXB)] + ["r%d" % b for b in range(MAXB)]
+              + ["arr%d" % j for j in range(NSLOT)] + ["a%d" % j for j in range(NSLOT)])
+
+
+def _plan(T, topo):
+    root = T.cores[T.root]
+    near = [c for c in T.cores if c != root and topo.may_write(root, c) and topo.may_write(c, root)]
+    far = [c for c in T.cores if c != root and c not in near]
+    proxy = {}
+    for f in far:
+        proxy[f] = [n for n in near if n not in proxy.values() and topo.may_write(f, n)
+                    and topo.chip(n) == topo.chip(f)][0]
+    order = [n for n in near if n not in proxy.values()] + [n for n in near if n in proxy.values()]
+    return root, far, proxy, order
+
+
+def _engines(mask):
+    return bin(mask).count("1")
+
+
+def rank_program(g, core, T, topo):
+    if T.rank_of(core) is None:
+        return
+    sem = T.sem
+    root, far, proxy, order = _plan(T, topo)
+    own = KB * W
+
+    if core in far:
+        p = proxy[core]
+        rid, pid = topo.addr(p, core)
+        m = topo.mask(core, p)
+        g.sync.dma_start(T.ks[:, 0:own], T.k[:, :]).then_inc(sem.ld_k, 16)
+        g.sync.dma_start(T.vs[:, 0:own], T.v[:, :]).then_inc(sem.ld_v, 16)
+        g.wait_ge(sem.ld_k, 16)
+        g.remote_dma(out_ap=T.ks[:, own:2 * own], in_ap=T.ks[:, 0:own], remote_sem=sem.k2_in, local_sem=sem.sent,
+                     pid=pid, routing_id=rid, dma_engine_mask=m)
+        g.wait_ge(sem.ld_v, 16)
+        g.remote_dma(out_ap=T.vs[:, own:2 * own], in_ap=T.vs[:, 0:own], remote_sem=sem.v2_in, local_sem=sem.sent,
+                     pid=pid, routing_id=rid, dma_engine_mask=m)
+        g.wait_ge(sem.sent, 2 * _engines(m))
+        return
+
+    guests = [f for f in far if proxy[f] == core]
+    nb = KB * (1 + len(guests))
+    tq, vq = g.tensor, g.vector
+    ps = [T.ps0, T.ps1, T.ps2, T.ps3]
+    po = T.po[:, 0:W]
+
+    if core == root:
+        g.sync.dma_start(T.qs[:, :], T.q[:, :]).then_inc(sem.q_in, 16)
+        g.sync.dma_start(T.ks[:, 0:own], T.k[:, :]).then_inc(sem.ld_k, 16)
+        g.sync.dma_start(T.vs[:, 0:own], T.v[:, :]).then_inc(sem.ld_v, 16)
+        q_n = 16
+        m = topo.mask(core, order[0])
+        for c in order:
+            m &= topo.mask(core, c)
+        ids = []
+        for c in order:
+            rid, pid = topo.addr(c, core)
+            ids.append(DstId(rid=rid, pnc=pid))
+        g.wait_ge(sem.q_in, 16)
+        g.remote_dma_fused([RemoteDMATransfer(dst_ids=ids, dma_engine_mask=m, remote_sem=sem.q_in,
+                                              srcs=[T.qs[:, :]], dsts=[T.qs[:, :] for c in order])],
+                           local_sem=sem.sent)
+        g.wait_ge(sem.sent, _engines(m))
+    else:
+        g.sync.dma_start(T.ks[:, 0:own], T.k[:, :]).then_inc(sem.ld_k, 16)
+        g.scalar.dma_start(T.vs[:, 0:own], T.v[:, :]).then_inc(sem.ld_v, 16)
+        q_n = _engines(topo.mask(root, core))
+
+    tq.wait_ge(sem.q_in, q_n)
+    for grp in range(nb // KB):
+        if grp == 0:
+            tq.wait_ge(sem.ld_k, 16)
+        else:
+            tq.wait_ge(sem.k2_in, _engines(topo.mask(guests[0], core)))
+        for b in range(grp * KB, grp * KB + KB):
+            tq.matmul(ps[b % NBANK][:, 0:W], T.ks[:, b * W:(b + 1) * W], T.qs[:, :], True, True).then_inc(
+                sem["s%d" % b], 1)
+        if grp == 0:
+            tq.wait_ge(sem.ld_v, 16)
+        else:
+            tq.wait_ge(sem.v2_in, _engines(topo.mask(guests[0], core)))
+        for b in range(grp * KB, grp * KB + KB):
+            tq.wait_ge(sem["r%d" % b], 1)
+            tq.matmul(po, T.vs[:, b * W:(b + 1) * W], T.ss[:, b * W:(b + 1) * W], b == 0, b == nb - 1).then_inc(
+                sem.o_done, 1)
+
+    vq.memset(T.zero[:, :], 0.0).then_inc(sem.zf, 1)
+    vq.wait_ge(sem.zf, 1)
+    for b in range(nb):
+        vq.wait_ge(sem["s%d" % b], 1)
+        vq.tensor_tensor(T.ss[:, b * W:(b + 1) * W], ps[b % NBANK][:, 0:W], T.zero[:, :], AluOpType.max).then_inc(
+            sem["r%d" % b], 1)
+    vq.wait_ge(sem.o_done, nb)
+
+    if core != root:
+        j = order.index(core)
+        vq.tensor_copy(T.ob[:, :], po).then_inc(sem.o_rdy, 1)
+        rid, pid = topo.addr(root, core)
+        m = topo.mask(core, root)
+        g.wait_ge(sem.o_rdy, 1)
+        g.remote_dma(out_ap=T.land[:, j * W:(j + 1) * W], in_ap=T.ob[:, :], remote_sem=sem["arr%d" % j],
+                     local_sem=sem.sent, pid=pid, routing_id=rid, dma_engine_mask=m)
+        g.wait_ge(sem.sent, _engines(m))
+        return
+
+    for j, c in enumerate(order):
+        last = j == len(order) - 1
+        vq.wait_ge(sem["arr%d" % j], _engines(topo.mask(c, core)))
+        vq.tensor_tensor(T.ob[:, :] if last else po, po, T.land[:, j * W:(j + 1) * W], AluOpType.add).then_inc(
+            sem["a%d" % j], 1)
+        if not last:
+            vq.wait_ge(sem["a%d" % j], 1)
+    g.sync.wait_ge(sem["a%d" % (len(order) - 1)], 1)
+    g.sync.dma_start(T.y[:, :], T.ob[:, :]).then_inc(sem.st, 16)
+    g.sync.wait_ge(sem.st, 16)

@@ -5,7 +5,7 @@ KB = 4
 W = 128
 NBANK = 4
 MAXB = 2 * KB
-NSLOT = 5
+NSLOT = 8
 
 SCRATCH = {
     "qs": ("sbuf", [128, W], "bfloat16"),
@@ -13,15 +13,16 @@ SCRATCH = {
     "vs": ("sbuf", [128, MAXB * W], "bfloat16"),
     "zero": ("sbuf", [128, W], "float32"),
     "ss": ("sbuf", [128, MAXB * W], "bfloat16"),
-    "ob": ("sbuf", [128, W], "bfloat16"),
+    "ob": ("sbuf", [128, 2 * W], "bfloat16"),
     "land": ("sbuf", [128, NSLOT * W], "bfloat16"),
     "ps0": ("psum", [128, 512], "float32"),
     "ps1": ("psum", [128, 512], "float32"),
     "ps2": ("psum", [128, 512], "float32"),
     "ps3": ("psum", [128, 512], "float32"),
-    "po": ("psum", [128, 512], "float32"),
+    "po0": ("psum", [128, 512], "float32"),
+    "po1": ("psum", [128, 512], "float32"),
 }
-SEMAPHORES = (["q_in", "ld_k", "ld_v", "k2_in", "v2_in", "sent", "zf", "o_done", "o_rdy", "st"]
+SEMAPHORES = (["q_in", "ld_k", "ld_v", "k2_in", "v2_in", "sent", "zf", "o_done0", "o_done1", "o_rdy0", "o_rdy1", "st"]
               + ["s%d" % b for b in range(MAXB)] + ["r%d" % b for b in range(MAXB)]
               + ["arr%d" % j for j in range(NSLOT)] + ["a%d" % j for j in range(NSLOT)])
 
@@ -34,8 +35,8 @@ def _plan(T, topo):
     for f in far:
         proxy[f] = [n for n in near if n not in proxy.values() and topo.may_write(f, n)
                     and topo.chip(n) == topo.chip(f)][0]
-    order = [n for n in near if n not in proxy.values()] + [n for n in near if n in proxy.values()]
-    return root, far, proxy, order
+    slots = [(n, 0) for n in near] + [(n, 1) for n in near if n in proxy.values()]
+    return root, near, far, proxy, slots
 
 
 def _engines(mask):
@@ -46,7 +47,7 @@ def rank_program(g, core, T, topo):
     if T.rank_of(core) is None:
         return
     sem = T.sem
-    root, far, proxy, order = _plan(T, topo)
+    root, near, far, proxy, slots = _plan(T, topo)
     own = KB * W
 
     if core in far:
@@ -65,26 +66,25 @@ def rank_program(g, core, T, topo):
         return
 
     guests = [f for f in far if proxy[f] == core]
-    nb = KB * (1 + len(guests))
+    ngrp = 1 + len(guests)
     tq, vq = g.tensor, g.vector
     ps = [T.ps0, T.ps1, T.ps2, T.ps3]
-    po = T.po[:, 0:W]
+    po = [T.po0[:, 0:W], T.po1[:, 0:W]]
 
     if core == root:
         g.sync.dma_start(T.qs[:, :], T.q[:, :]).then_inc(sem.q_in, 16)
         g.sync.dma_start(T.ks[:, 0:own], T.k[:, :]).then_inc(sem.ld_k, 16)
         g.sync.dma_start(T.vs[:, 0:own], T.v[:, :]).then_inc(sem.ld_v, 16)
         q_n = 16
-        m = topo.mask(core, order[0])
-        for c in order:
-            m &= topo.mask(core, c)
+        m = topo.mask(core, near[0])
         ids = []
-        for c in order:
+        for c in near:
+            m &= topo.mask(core, c)
             rid, pid = topo.addr(c, core)
             ids.append(DstId(rid=rid, pnc=pid))
         g.wait_ge(sem.q_in, 16)
         g.remote_dma_fused([RemoteDMATransfer(dst_ids=ids, dma_engine_mask=m, remote_sem=sem.q_in,
-                                              srcs=[T.qs[:, :]], dsts=[T.qs[:, :] for c in order])],
+                                              srcs=[T.qs[:, :]], dsts=[T.qs[:, :] for c in near])],
                            local_sem=sem.sent)
         g.wait_ge(sem.sent, _engines(m))
     else:
@@ -93,7 +93,7 @@ def rank_program(g, core, T, topo):
         q_n = _engines(topo.mask(root, core))
 
     tq.wait_ge(sem.q_in, q_n)
-    for grp in range(nb // KB):
+    for grp in range(ngrp):
         if grp == 0:
             tq.wait_ge(sem.ld_k, 16)
         else:
@@ -107,35 +107,39 @@ def rank_program(g, core, T, topo):
             tq.wait_ge(sem.v2_in, _engines(topo.mask(guests[0], core)))
         for b in range(grp * KB, grp * KB + KB):
             tq.wait_ge(sem["r%d" % b], 1)
-            tq.matmul(po, T.vs[:, b * W:(b + 1) * W], T.ss[:, b * W:(b + 1) * W], b == 0, b == nb - 1).then_inc(
-                sem.o_done, 1)
+            tq.matmul(po[grp], T.vs[:, b * W:(b + 1) * W], T.ss[:, b * W:(b + 1) * W], b % KB == 0,
+                      b % KB == KB - 1).then_inc(sem["o_done%d" % grp], 1)
 
     vq.memset(T.zero[:, :], 0.0).then_inc(sem.zf, 1)
     vq.wait_ge(sem.zf, 1)
-    for b in range(nb):
-        vq.wait_ge(sem["s%d" % b], 1)
-        vq.tensor_tensor(T.ss[:, b * W:(b + 1) * W], ps[b % NBANK][:, 0:W], T.zero[:, :], AluOpType.max).then_inc(
-            sem["r%d" % b], 1)
-    vq.wait_ge(sem.o_done, nb)
+    for grp in range(ngrp):
+        for b in range(grp * KB, grp * KB + KB):
+            vq.wait_ge(sem["s%d" % b], 1)
+            vq.tensor_tensor(T.ss[:, b * W:(b + 1) * W], ps[b % NBANK][:, 0:W], T.zero[:, :],
+                             AluOpType.max).then_inc(sem["r%d" % b], 1)
+        vq.wait_ge(sem["o_done%d" % grp], KB)
+        if core != root:
+            vq.tensor_copy(T.ob[:, grp * W:(grp + 1) * W], po[grp]).then_inc(sem["o_rdy%d" % grp], 1)
 
     if core != root:
-        j = order.index(core)
-        vq.tensor_copy(T.ob[:, :], po).then_inc(sem.o_rdy, 1)
         rid, pid = topo.addr(root, core)
         m = topo.mask(core, root)
-        g.wait_ge(sem.o_rdy, 1)
-        g.remote_dma(out_ap=T.land[:, j * W:(j + 1) * W], in_ap=T.ob[:, :], remote_sem=sem["arr%d" % j],
-                     local_sem=sem.sent, pid=pid, routing_id=rid, dma_engine_mask=m)
-        g.wait_ge(sem.sent, _engines(m))
+        for grp in range(ngrp):
+            j = slots.index((core, grp))
+            g.wait_ge(sem["o_rdy%d" % grp], 1)
+            g.remote_dma(out_ap=T.land[:, j * W:(j + 1) * W], in_ap=T.ob[:, grp * W:(grp + 1) * W],
+                         remote_sem=sem["arr%d" % j], local_sem=sem.sent, pid=pid, routing_id=rid,
+                         dma_engine_mask=m)
+        g.wait_ge(sem.sent, ngrp * _engines(m))
         return
 
-    for j, c in enumerate(order):
-        last = j == len(order) - 1
+    for j, (c, grp) in enumerate(slots):
+        last = j == len(slots) - 1
         vq.wait_ge(sem["arr%d" % j], _engines(topo.mask(c, core)))
-        vq.tensor_tensor(T.ob[:, :] if last else po, po, T.land[:, j * W:(j + 1) * W], AluOpType.add).then_inc(
-            sem["a%d" % j], 1)
+        vq.tensor_tensor(T.ob[:, 0:W] if last else po[0], po[0], T.land[:, j * W:(j + 1) * W],
+                         AluOpType.add).then_inc(sem["a%d" % j], 1)
         if not last:
             vq.wait_ge(sem["a%d" % j], 1)
-    g.sync.wait_ge(sem["a%d" % (len(order) - 1)], 1)
-    g.sync.dma_start(T.y[:, :], T.ob[:, :]).then_inc(sem.st, 16)
+    g.sync.wait_ge(sem["a%d" % (len(slots) - 1)], 1)
+    g.sync.dma_start(T.y[:, :], T.ob[:, 0:W]).then_inc(sem.st, 16)
     g.sync.wait_ge(sem.st, 16)

@@ -6,6 +6,8 @@ W = 128
 NBANK = 4
 MAXB = 2 * KB
 NSLOT = 8
+NCAR = 2
+WORLD = 512
 
 SCRATCH = {
     "qs": ("sbuf", [128, W], "bfloat16"),
@@ -22,7 +24,8 @@ SCRATCH = {
     "po0": ("psum", [128, 512], "float32"),
     "po1": ("psum", [128, 512], "float32"),
 }
-SEMAPHORES = (["q_in", "ld_k", "ld_v", "k2_in", "v2_in", "sent", "zf", "o_done0", "o_done1", "o_rdy0", "o_rdy1", "st"]
+SEMAPHORES = (["q_in", "ld_k", "ld_v", "k2_in", "v_car", "sent", "zf", "o_done0", "o_done1", "o_rdy0", "o_rdy1", "st"]
+              + ["v2_in%d" % i for i in range(NCAR)]
               + ["s%d" % b for b in range(MAXB)] + ["r%d" % b for b in range(MAXB)]
               + ["arr%d" % j for j in range(NSLOT)] + ["a%d" % j for j in range(NSLOT)])
 
@@ -36,33 +39,73 @@ def _plan(T, topo):
         proxy[f] = [n for n in near if n not in proxy.values() and topo.may_write(f, n)
                     and topo.chip(n) == topo.chip(f)][0]
     slots = [(n, 0) for n in near] + [(n, 1) for n in near if n in proxy.values()]
-    return root, near, far, proxy, slots
+    carriers = {}
+    for f in far:
+        chipmates = [x for x in range(WORLD) if topo.host(x) == topo.host(f) and topo.chip(x) == topo.chip(f)]
+        mate = [x for x in range(WORLD) if topo.mates(f, x)][0]
+
+        def pair(x):
+            return (topo.die(x), topo.may_write(x, mate))
+        chosen = []
+        for x in sorted(chipmates, key=lambda x: topo.die(x) != topo.die(f)):
+            if pair(x) != pair(f) and pair(x) not in [pair(h) for h in chosen] and topo.may_write(x, proxy[f]):
+                chosen.append(x)
+        carriers[f] = chosen[:NCAR]
+    return root, near, far, proxy, slots, carriers
 
 
 def _engines(mask):
     return bin(mask).count("1")
 
 
+def _parts(mask, n):
+    bits = [i for i in range(mask.bit_length()) if (mask >> i) & 1]
+    k = len(bits) // n
+    return [sum(1 << i for i in bits[j * k:(j + 1) * k]) for j in range(n)]
+
+
 def rank_program(g, core, T, topo):
+    sem = T.sem
+    root, near, far, proxy, slots, carriers = _plan(T, topo)
+    own = KB * W
+    part = own // NCAR
+
+    for f in far:
+        if core in carriers[f]:
+            i = carriers[f].index(core)
+            n_in = _engines(_parts(topo.mask(f, core) & ~topo.mask(f, proxy[f]), NCAR)[i])
+            rid, pid = topo.addr(proxy[f], core)
+            m = topo.mask(core, proxy[f])
+            g.wait_ge(sem.v_car, n_in)
+            g.remote_dma(out_ap=T.vs[:, own + i * part:own + (i + 1) * part], in_ap=T.vs[:, i * part:(i + 1) * part],
+                         remote_sem=sem["v2_in%d" % i], local_sem=sem.sent, pid=pid, routing_id=rid,
+                         dma_engine_mask=m)
+            g.wait_ge(sem.sent, _engines(m))
+            return
     if T.rank_of(core) is None:
         return
-    sem = T.sem
-    root, near, far, proxy, slots = _plan(T, topo)
-    own = KB * W
 
     if core in far:
         p = proxy[core]
-        rid, pid = topo.addr(p, core)
         m = topo.mask(core, p)
-        g.sync.dma_start(T.ks[:, 0:own], T.k[:, :]).then_inc(sem.ld_k, 16)
         g.sync.dma_start(T.vs[:, 0:own], T.v[:, :]).then_inc(sem.ld_v, 16)
+        g.scalar.dma_start(T.ks[:, 0:own], T.k[:, :]).then_inc(sem.ld_k, 16)
+        trs = []
+        n_loc = 0
+        for i, h in enumerate(carriers[core]):
+            rid, pid = topo.addr(h, core)
+            mi = _parts(topo.mask(core, h) & ~m, NCAR)[i]
+            n_loc += _engines(mi)
+            trs.append(RemoteDMATransfer(dst_ids=[DstId(rid=rid, pnc=pid)], dma_engine_mask=mi, remote_sem=sem.v_car,
+                                         srcs=[T.vs[:, i * part:(i + 1) * part]],
+                                         dsts=[T.vs[:, i * part:(i + 1) * part]]))
+        g.wait_ge(sem.ld_v, 16)
+        g.remote_dma_fused(trs, local_sem=sem.sent)
+        rid, pid = topo.addr(p, core)
         g.wait_ge(sem.ld_k, 16)
         g.remote_dma(out_ap=T.ks[:, own:2 * own], in_ap=T.ks[:, 0:own], remote_sem=sem.k2_in, local_sem=sem.sent,
                      pid=pid, routing_id=rid, dma_engine_mask=m)
-        g.wait_ge(sem.ld_v, 16)
-        g.remote_dma(out_ap=T.vs[:, own:2 * own], in_ap=T.vs[:, 0:own], remote_sem=sem.v2_in, local_sem=sem.sent,
-                     pid=pid, routing_id=rid, dma_engine_mask=m)
-        g.wait_ge(sem.sent, 2 * _engines(m))
+        g.wait_ge(sem.sent, n_loc + _engines(m))
         return
 
     guests = [f for f in far if proxy[f] == core]
@@ -103,9 +146,10 @@ def rank_program(g, core, T, topo):
                 sem["s%d" % b], 1)
         if grp == 0:
             tq.wait_ge(sem.ld_v, 16)
-        else:
-            tq.wait_ge(sem.v2_in, _engines(topo.mask(guests[0], core)))
         for b in range(grp * KB, grp * KB + KB):
+            if grp == 1 and (b % KB) % (KB // NCAR) == 0:
+                i = (b % KB) // (KB // NCAR)
+                tq.wait_ge(sem["v2_in%d" % i], _engines(topo.mask(carriers[guests[0]][i], core)))
             tq.wait_ge(sem["r%d" % b], 1)
             tq.matmul(po[grp], T.vs[:, b * W:(b + 1) * W], T.ss[:, b * W:(b + 1) * W], b % KB == 0,
                       b % KB == KB - 1).then_inc(sem["o_done%d" % grp], 1)

@@ -7,12 +7,14 @@ NBANK = 4
 MAXB = 2 * KB
 NSLOT = 8
 NCAR = 2
+KD = KB - 1
 WORLD = 512
 
 SCRATCH = {
     "qs": ("sbuf", [128, W], "bfloat16"),
     "ks": ("sbuf", [128, MAXB * W], "bfloat16"),
     "vs": ("sbuf", [128, MAXB * W], "bfloat16"),
+    "vd": ("dram", [NCAR, 128, KB * W // NCAR], "bfloat16"),
     "zero": ("sbuf", [128, W], "float32"),
     "ss": ("sbuf", [128, MAXB * W], "bfloat16"),
     "ob": ("sbuf", [128, 2 * W], "bfloat16"),
@@ -24,7 +26,8 @@ SCRATCH = {
     "po0": ("psum", [128, 512], "float32"),
     "po1": ("psum", [128, 512], "float32"),
 }
-SEMAPHORES = (["q_in", "ld_k", "ld_v", "k2_in", "v_car", "sent", "zf", "o_done0", "o_done1", "o_rdy0", "o_rdy1", "st"]
+SEMAPHORES = (["q_in", "ld_k", "ld_v", "k2_in", "k3_in", "car", "sent", "zf", "o_done0", "o_done1", "o_rdy0", "o_rdy1",
+               "st"]
               + ["v2_in%d" % i for i in range(NCAR)]
               + ["s%d" % b for b in range(MAXB)] + ["r%d" % b for b in range(MAXB)]
               + ["arr%d" % j for j in range(NSLOT)] + ["a%d" % j for j in range(NSLOT)])
@@ -38,6 +41,7 @@ def _plan(T, topo):
     for f in far:
         proxy[f] = [n for n in near if n not in proxy.values() and topo.may_write(f, n)
                     and topo.chip(n) == topo.chip(f)][0]
+    near = [n for n in near if n in proxy.values()] + [n for n in near if n not in proxy.values()]
     slots = [(n, 0) for n in near] + [(n, 1) for n in near if n in proxy.values()]
     carriers = {}
     for f in far:
@@ -50,7 +54,7 @@ def _plan(T, topo):
         for x in sorted(chipmates, key=lambda x: topo.die(x) != topo.die(f)):
             if pair(x) != pair(f) and pair(x) not in [pair(h) for h in chosen] and topo.may_write(x, proxy[f]):
                 chosen.append(x)
-        carriers[f] = chosen[:NCAR]
+        carriers[f] = chosen[:NCAR + 1]
     return root, near, far, proxy, slots, carriers
 
 
@@ -69,17 +73,25 @@ def rank_program(g, core, T, topo):
     root, near, far, proxy, slots, carriers = _plan(T, topo)
     own = KB * W
     part = own // NCAR
+    kd = KD * W
+
+    def hand_mask(f, i):
+        return _parts(topo.mask(f, carriers[f][i]) & ~topo.mask(f, proxy[f]), NCAR)[i % NCAR]
 
     for f in far:
         if core in carriers[f]:
             i = carriers[f].index(core)
-            n_in = _engines(_parts(topo.mask(f, core) & ~topo.mask(f, proxy[f]), NCAR)[i])
             rid, pid = topo.addr(proxy[f], core)
             m = topo.mask(core, proxy[f])
-            g.wait_ge(sem.v_car, n_in)
-            g.remote_dma(out_ap=T.vs[:, own + i * part:own + (i + 1) * part], in_ap=T.vs[:, i * part:(i + 1) * part],
-                         remote_sem=sem["v2_in%d" % i], local_sem=sem.sent, pid=pid, routing_id=rid,
-                         dma_engine_mask=m)
+            g.wait_ge(sem.car, _engines(hand_mask(f, i)))
+            if i < NCAR:
+                g.remote_dma(out_ap=T.vs[:, own + i * part:own + (i + 1) * part], in_ap=T.vd[i],
+                             remote_sem=sem["v2_in%d" % i], local_sem=sem.sent, pid=pid, routing_id=rid,
+                             dma_engine_mask=m)
+            else:
+                g.remote_dma(out_ap=T.ks[:, own + kd:2 * own], in_ap=T.ks[:, kd:own],
+                             remote_sem=sem.k3_in, local_sem=sem.sent, pid=pid, routing_id=rid,
+                             dma_engine_mask=m)
             g.wait_ge(sem.sent, _engines(m))
             return
     if T.rank_of(core) is None:
@@ -88,24 +100,27 @@ def rank_program(g, core, T, topo):
     if core in far:
         p = proxy[core]
         m = topo.mask(core, p)
-        g.sync.dma_start(T.vs[:, 0:own], T.v[:, :]).then_inc(sem.ld_v, 16)
-        g.scalar.dma_start(T.ks[:, 0:own], T.k[:, :]).then_inc(sem.ld_k, 16)
+        lq = [g.sync, g.scalar]
+        for i in range(NCAR):
+            lq[i % 2].dma_start(T.vd[i], T.v[:, i * part:(i + 1) * part]).then_inc(sem.ld_v, 16)
+        g.sync.dma_start(T.ks[:, 0:own], T.k[:, :]).then_inc(sem.ld_k, 16)
         trs = []
         n_loc = 0
-        for i, h in enumerate(carriers[core]):
-            rid, pid = topo.addr(h, core)
-            mi = _parts(topo.mask(core, h) & ~m, NCAR)[i]
-            n_loc += _engines(mi)
-            trs.append(RemoteDMATransfer(dst_ids=[DstId(rid=rid, pnc=pid)], dma_engine_mask=mi, remote_sem=sem.v_car,
-                                         srcs=[T.vs[:, i * part:(i + 1) * part]],
-                                         dsts=[T.vs[:, i * part:(i + 1) * part]]))
-        g.wait_ge(sem.ld_v, 16)
+        for i in range(NCAR):
+            rid, pid = topo.addr(carriers[core][i], core)
+            n_loc += _engines(hand_mask(core, i))
+            trs.append(RemoteDMATransfer(dst_ids=[DstId(rid=rid, pnc=pid)], dma_engine_mask=hand_mask(core, i),
+                                         remote_sem=sem.car, srcs=[T.vd[i]], dsts=[T.vd[i]]))
+        g.wait_ge(sem.ld_v, 16 * NCAR)
         g.remote_dma_fused(trs, local_sem=sem.sent)
         rid, pid = topo.addr(p, core)
         g.wait_ge(sem.ld_k, 16)
-        g.remote_dma(out_ap=T.ks[:, own:2 * own], in_ap=T.ks[:, 0:own], remote_sem=sem.k2_in, local_sem=sem.sent,
+        g.remote_dma(out_ap=T.ks[:, own:own + kd], in_ap=T.ks[:, 0:kd], remote_sem=sem.k2_in, local_sem=sem.sent,
                      pid=pid, routing_id=rid, dma_engine_mask=m)
-        g.wait_ge(sem.sent, n_loc + _engines(m))
+        rid, pid = topo.addr(carriers[core][NCAR], core)
+        g.remote_dma(out_ap=T.ks[:, kd:own], in_ap=T.ks[:, kd:own], remote_sem=sem.car, local_sem=sem.sent,
+                     pid=pid, routing_id=rid, dma_engine_mask=hand_mask(core, NCAR))
+        g.wait_ge(sem.sent, n_loc + _engines(m) + _engines(hand_mask(core, NCAR)))
         return
 
     guests = [f for f in far if proxy[f] == core]
@@ -142,6 +157,8 @@ def rank_program(g, core, T, topo):
         else:
             tq.wait_ge(sem.k2_in, _engines(topo.mask(guests[0], core)))
         for b in range(grp * KB, grp * KB + KB):
+            if grp == 1 and b % KB == KD:
+                tq.wait_ge(sem.k3_in, _engines(topo.mask(carriers[guests[0]][NCAR], core)))
             tq.matmul(ps[b % NBANK][:, 0:W], T.ks[:, b * W:(b + 1) * W], T.qs[:, :], True, True).then_inc(
                 sem["s%d" % b], 1)
         if grp == 0:

from concourse.bass import DstId, RemoteDMATransfer
from concourse.mybir import AluOpType

KB = 4
W = 128
NBANK = 4
MAXB = 2 * KB
NSLOT = 8
NCAR = 2
KD = KB - 1
WORLD = 512

SCRATCH = {
    "qs": ("sbuf", [128, W], "bfloat16"),
    "ks": ("sbuf", [128, MAXB * W], "bfloat16"),
    "vs": ("sbuf", [128, MAXB * W], "bfloat16"),
    "vd": ("dram", [NCAR, 128, KB * W // NCAR], "bfloat16"),
    "zero": ("sbuf", [128, W], "float32"),
    "ss": ("sbuf", [128, MAXB * W], "bfloat16"),
    "ob": ("sbuf", [128, 2 * W], "bfloat16"),
    "land": ("sbuf", [128, NSLOT * W], "bfloat16"),
    "ps0": ("psum", [128, 512], "float32"),
    "ps1": ("psum", [128, 512], "float32"),
    "ps2": ("psum", [128, 512], "float32"),
    "ps3": ("psum", [128, 512], "float32"),
    "po0": ("psum", [128, 512], "float32"),
    "po1": ("psum", [128, 512], "float32"),
}
SEMAPHORES = (["q_in", "ld_k", "ld_v", "k2_in", "k3_in", "car", "sent", "zf", "o_done0", "o_done1", "o_rdy0", "o_rdy1",
               "st"]
              + ["v2_in%d" % i for i in range(NCAR)]
              + ["s%d" % b for b in range(MAXB)] + ["r%d" % b for b in range(MAXB)]
              + ["arr%d" % j for j in range(NSLOT)] + ["a%d" % j for j in range(NSLOT)])


def _plan(T, topo):
    root = T.cores[T.root]
    near = [c for c in T.cores if c != root and topo.may_write(root, c) and topo.may_write(c, root)]
    far = [c for c in T.cores if c != root and c not in near]
    proxy = {}
    for f in far:
        proxy[f] = [n for n in near if n not in proxy.values() and topo.may_write(f, n)
                    and topo.chip(n) == topo.chip(f)][0]
    near = [n for n in near if n in proxy.values()] + [n for n in near if n not in proxy.values()]
    slots = [(n, 0) for n in near] + [(n, 1) for n in near if n in proxy.values()]
    carriers = {}
    for f in far:
        chipmates = [x for x in range(WORLD) if topo.host(x) == topo.host(f) and topo.chip(x) == topo.chip(f)]
        mate = [x for x in range(WORLD) if topo.mates(f, x)][0]

        def pair(x):
            return (topo.die(x), topo.may_write(x, mate))
        chosen = []
        for x in sorted(chipmates, key=lambda x: topo.die(x) != topo.die(f)):
            if pair(x) != pair(f) and pair(x) not in [pair(h) for h in chosen] and topo.may_write(x, proxy[f]):
                chosen.append(x)
        carriers[f] = chosen[:NCAR + 1]
    return root, near, far, proxy, slots, carriers


def _engines(mask):
    return bin(mask).count("1")


def _parts(mask, n):
    bits = [i for i in range(mask.bit_length()) if (mask >> i) & 1]
    k = len(bits) // n
    return [sum(1 << i for i in bits[j * k:(j + 1) * k]) for j in range(n)]


def rank_program(g, core, T, topo):
    sem = T.sem
    root, near, far, proxy, slots, carriers = _plan(T, topo)
    own = KB * W
    part = own // NCAR
    kd = KD * W

    def hand_mask(f, i):
        return _parts(topo.mask(f, carriers[f][i]) & ~topo.mask(f, proxy[f]), NCAR)[i % NCAR]

    for f in far:
        if core in carriers[f]:
            i = carriers[f].index(core)
            rid, pid = topo.addr(proxy[f], core)
            m = topo.mask(core, proxy[f])
            g.wait_ge(sem.car, _engines(hand_mask(f, i)))
            if i < NCAR:
                g.remote_dma(out_ap=T.vs[:, own + i * part:own + (i + 1) * part], in_ap=T.vd[i],
                             remote_sem=sem["v2_in%d" % i], local_sem=sem.sent, pid=pid, routing_id=rid,
                             dma_engine_mask=m)
            else:
                g.remote_dma(out_ap=T.ks[:, own + kd:2 * own], in_ap=T.ks[:, kd:own],
                             remote_sem=sem.k3_in, local_sem=sem.sent, pid=pid, routing_id=rid,
                             dma_engine_mask=m)
            g.wait_ge(sem.sent, _engines(m))
            return
    if T.rank_of(core) is None:
        return

    if core in far:
        p = proxy[core]
        m = topo.mask(core, p)
        lq = [g.sync, g.scalar]
        for i in range(NCAR):
            lq[i % 2].dma_start(T.vd[i], T.v[:, i * part:(i + 1) * part]).then_inc(sem.ld_v, 16)
        g.sync.dma_start(T.ks[:, 0:own], T.k[:, :]).then_inc(sem.ld_k, 16)
        trs = []
        n_loc = 0
        for i in range(NCAR):
            rid, pid = topo.addr(carriers[core][i], core)
            n_loc += _engines(hand_mask(core, i))
            trs.append(RemoteDMATransfer(dst_ids=[DstId(rid=rid, pnc=pid)], dma_engine_mask=hand_mask(core, i),
                                         remote_sem=sem.car, srcs=[T.vd[i]], dsts=[T.vd[i]]))
        g.wait_ge(sem.ld_v, 16 * NCAR)
        g.remote_dma_fused(trs, local_sem=sem.sent)
        rid, pid = topo.addr(p, core)
        g.wait_ge(sem.ld_k, 16)
        g.remote_dma(out_ap=T.ks[:, own:own + kd], in_ap=T.ks[:, 0:kd], remote_sem=sem.k2_in, local_sem=sem.sent,
                     pid=pid, routing_id=rid, dma_engine_mask=m)
        rid, pid = topo.addr(carriers[core][NCAR], core)
        g.remote_dma(out_ap=T.ks[:, kd:own], in_ap=T.ks[:, kd:own], remote_sem=sem.car, local_sem=sem.sent,
                     pid=pid, routing_id=rid, dma_engine_mask=hand_mask(core, NCAR))
        g.wait_ge(sem.sent, n_loc + _engines(m) + _engines(hand_mask(core, NCAR)))
        return

    guests = [f for f in far if proxy[f] == core]
    ngrp = 1 + len(guests)
    tq, vq = g.tensor, g.vector
    ps = [T.ps0, T.ps1, T.ps2, T.ps3]
    po = [T.po0[:, 0:W], T.po1[:, 0:W]]

    if core == root:
        g.sync.dma_start(T.qs[:, :], T.q[:, :]).then_inc(sem.q_in, 16)
        g.sync.dma_start(T.ks[:, 0:own], T.k[:, :]).then_inc(sem.ld_k, 16)
        g.sync.dma_start(T.vs[:, 0:own], T.v[:, :]).then_inc(sem.ld_v, 16)
        q_n = 16
        m = topo.mask(core, near[0])
        ids = []
        for c in near:
            m &= topo.mask(core, c)
            rid, pid = topo.addr(c, core)
            ids.append(DstId(rid=rid, pnc=pid))
        g.wait_ge(sem.q_in, 16)
        g.remote_dma_fused([RemoteDMATransfer(dst_ids=ids, dma_engine_mask=m, remote_sem=sem.q_in,
                                              srcs=[T.qs[:, :]], dsts=[T.qs[:, :] for c in near])],
                           local_sem=sem.sent)
        g.wait_ge(sem.sent, _engines(m))
    else:
        g.sync.dma_start(T.ks[:, 0:own], T.k[:, :]).then_inc(sem.ld_k, 16)
        g.scalar.dma_start(T.vs[:, 0:own], T.v[:, :]).then_inc(sem.ld_v, 16)
        q_n = _engines(topo.mask(root, core))

    tq.wait_ge(sem.q_in, q_n)
    for grp in range(ngrp):
        if grp == 0:
            tq.wait_ge(sem.ld_k, 16)
        else:
            tq.wait_ge(sem.k2_in, _engines(topo.mask(guests[0], core)))
        for b in range(grp * KB, grp * KB + KB):
            if grp == 1 and b % KB == KD:
                tq.wait_ge(sem.k3_in, _engines(topo.mask(carriers[guests[0]][NCAR], core)))
            tq.matmul(ps[b % NBANK][:, 0:W], T.ks[:, b * W:(b + 1) * W], T.qs[:, :], True, True).then_inc(
                sem["s%d" % b], 1)
        if grp == 0:
            tq.wait_ge(sem.ld_v, 16)
        for b in range(grp * KB, grp * KB + KB):
            if grp == 1 and (b % KB) % (KB // NCAR) == 0:
                i = (b % KB) // (KB // NCAR)
                tq.wait_ge(sem["v2_in%d" % i], _engines(topo.mask(carriers[guests[0]][i], core)))
            tq.wait_ge(sem["r%d" % b], 1)
            tq.matmul(po[grp], T.vs[:, b * W:(b + 1) * W], T.ss[:, b * W:(b + 1) * W], b % KB == 0,
                      b % KB == KB - 1).then_inc(sem["o_done%d" % grp], 1)

    vq.memset(T.zero[:, :], 0.0).then_inc(sem.zf, 1)
    vq.wait_ge(sem.zf, 1)
    for grp in range(ngrp):
        for b in range(grp * KB, grp * KB + KB):
            vq.wait_ge(sem["s%d" % b], 1)
            vq.tensor_tensor(T.ss[:, b * W:(b + 1) * W], ps[b % NBANK][:, 0:W], T.zero[:, :],
                             AluOpType.max).then_inc(sem["r%d" % b], 1)
        vq.wait_ge(sem["o_done%d" % grp], KB)
        if core != root:
            vq.tensor_copy(T.ob[:, grp * W:(grp + 1) * W], po[grp]).then_inc(sem["o_rdy%d" % grp], 1)

    if core != root:
        rid, pid = topo.addr(root, core)
        m = topo.mask(core, root)
        for grp in range(ngrp):
            j = slots.index((core, grp))
            g.wait_ge(sem["o_rdy%d" % grp], 1)
            g.remote_dma(out_ap=T.land[:, j * W:(j + 1) * W], in_ap=T.ob[:, grp * W:(grp + 1) * W],
                         remote_sem=sem["arr%d" % j], local_sem=sem.sent, pid=pid, routing_id=rid,
                         dma_engine_mask=m)
        g.wait_ge(sem.sent, ngrp * _engines(m))
        return

    for j, (c, grp) in enumerate(slots):
        last = j == len(slots) - 1
        vq.wait_ge(sem["arr%d" % j], _engines(topo.mask(c, core)))
        vq.tensor_tensor(T.ob[:, 0:W] if last else po[0], po[0], T.land[:, j * W:(j + 1) * W],
                         AluOpType.add).then_inc(sem["a%d" % j], 1)
        if not last:
            vq.wait_ge(sem["a%d" % j], 1)
    g.sync.wait_ge(sem["a%d" % (len(slots) - 1)], 1)
    g.sync.dma_start(T.y[:, :], T.ob[:, 0:W]).then_inc(sem.st, 16)
    g.sync.wait_ge(sem.st, 16)
